import numpy as np
import ml_dtypes


def mxq(x, axis, fmt="e4m3"):
    dtype, down = {"e4m3": (ml_dtypes.float8_e4m3fn, 7), "e5m2": (ml_dtypes.float8_e5m2, 14)}[fmt]
    v = np.moveaxis(np.asarray(x, np.float32).astype(ml_dtypes.bfloat16).astype(np.float64), axis, -1)
    blocks = v.reshape(v.shape[:-1] + (-1, 32))
    amax = np.abs(blocks).max(-1, keepdims=True)
    byte = np.maximum(np.where(amax > 0, np.frexp(amax)[1] - 1 + 127, 0) - down, 1)
    scale = np.exp2(byte - 127.0)
    codes = (blocks / scale).astype(np.float32).astype(dtype).astype(np.float64)
    return np.moveaxis((codes * scale).reshape(v.shape), -1, axis)


WIDE = False


def mx_kscale(k):
    if not WIDE:
        return np.ones(k)
    levels = np.array([10, -10, 5, -5, 0])
    if k % 512:
        return np.exp2(np.random.permutation(np.resize(levels, k // 32))).repeat(32)
    a = np.empty((k // 512, 16))
    for p in range(k // 512):
        a[p, :8] = np.random.permutation(np.resize(levels, 8))
        for g in range(8):
            far = levels[np.abs(levels - a[p, g]) >= 10]
            a[p, g + 8] = far[np.random.randint(len(far))]
    return np.exp2(a.ravel()).repeat(32)


def f64(x):
    return np.asarray(x).astype(np.float64)


def striped8(idx):
    return np.concatenate([x.reshape(-1, 16).T for x in idx]).astype(np.uint16)


def runs(offs, k):
    lists = np.stack([offs[16 * r : 16 * r + 16].T.reshape(-1) for r in range(8)]).astype(np.int64)
    return lists[np.arange(k) % 512 // 64]


def pack_weight(w):
    k, n = w.shape
    w = f64(np.asarray(w, np.float32).astype(ml_dtypes.bfloat16)).reshape(k // 32, 32, n)
    amax = np.abs(w).max(1)
    byte = np.clip(np.where(amax > 0, np.frexp(amax)[1] - 1 + 127 - 7, 1), 1, 254)
    scaled = (w * np.exp2(127.0 - byte)[:, None, :]).reshape(k, n).astype(np.float32)
    words = np.ascontiguousarray(scaled.reshape(k // 512, 128, 4, n).transpose(0, 1, 3, 2)).astype(ml_dtypes.float8_e4m3fn).view(np.uint8)
    return words, np.ascontiguousarray(byte.astype(np.uint8).reshape(k // 512, 16, n))


def unpack_weight(words, scales):
    g, p, n, _ = words.shape
    vals = np.ascontiguousarray(words).view(ml_dtypes.float8_e4m3fn).astype(np.float64) * np.repeat(np.exp2(scales.astype(np.float64) - 127.0), 8, axis=1)[..., None]
    return vals.transpose(0, 1, 3, 2).reshape(g * 512, n)


def sigmoid(v):
    return 1.0 / (1.0 + np.exp(-np.maximum(v, -700.0)))


K, T, S, N = 1024, 2048, 512, 256


def setup_inputs():
    n = np.random.standard_normal
    s = mx_kscale(K)[:, None]
    packed_xT = pack_weight(n((K, T)) * s)
    return {
        "x_words": packed_xT[0],
        "x_scales": packed_xT[1],
        "w1": (n((K, N)) / np.sqrt(K) / s).astype(np.float32),
        "w2": (n((K, N)) / np.sqrt(K) / s).astype(np.float32),
        "st": n((N, S)).astype(np.float32),
        "offs": striped8(np.stack([np.random.permutation(T)[:S] for _ in range(8)])),
    }


def reference(x_words, x_scales, w1, w2, st, offs):
    xq = unpack_weight(x_words, x_scales)[np.arange(K)[:, None], runs(offs, K)]
    f = sigmoid(mxq(f64(w1), 0, "e4m3").T @ xq)
    g = np.tanh(mxq(f64(w2), 0, "e4m3").T @ xq)
    return f64(st) + f * (g - f64(st))

@@ -1,0 +1,205 @@
+from contextlib import ExitStack
+
+import concourse.mybir as mybir
+
+K, T, S, N = 1024, 2048, 512, 256
+FLOPS = 2 * 2 * K * S * N
+
+F32 = mybir.dt.float32
+BF16 = mybir.dt.bfloat16
+I32 = mybir.dt.int32
+U32 = mybir.dt.uint32
+U16 = mybir.dt.uint16
+U8 = mybir.dt.uint8
+FP8X4 = mybir.dt.float8_e4m3fn_x4
+TANH = mybir.ActivationFunctionType.Tanh
+ADD = mybir.AluOpType.add
+SUB = mybir.AluOpType.subtract
+MULT = mybir.AluOpType.mult
+
+P = 128
+PACK = 4
+K_PASS = P * PACK
+PASSES = K // K_PASS
+HALF = S // 2
+PLANE = 8
+PIECE = PACK * P
+
+
+def tile_picked_phcell_none_p_kernel(tc, x_words, x_scales, w1, w2, st, offs, out):
+    nc = tc.nc
+    weights = {"f": w1, "g": w2}
+    with ExitStack() as ctx:
+        keep = ctx.enter_context(tc.tile_pool(name="keep", bufs=1))
+        psum = ctx.enter_context(tc.psum_pool(name="psum", bufs=1))
+
+        scale_table = keep.tile([P, T], U8, name="scale_table", align_bytes=64)
+        nc.vector.memset(scale_table[:, : 3 * T // 4].bitcast(I32), 0)
+        nc.gpsimd.memset(scale_table[:, 3 * T // 4 :].bitcast(I32), 0)
+
+        offsets = keep.tile([P, S // 16], U16, name="offsets")
+        nc.sync.dma_start(offsets[:], offs)
+
+        def load_words(a):
+            t = keep.tile([P, T], U32, name="word_table%d" % a, align_bytes=64)
+            nc.sync.dma_start(t[:].bitcast(I32), x_words[a].rearrange("p c r -> p (c r)").bitcast(I32))
+            return t
+
+        raw = {}
+        state = {}
+
+        def load_w(name, a, m, dst):
+            rows = weights[name][a * K_PASS : (a + 1) * K_PASS, m * P : (m + 1) * P]
+            nc.sync.dma_start(dst.rearrange("p (j c) -> p j c", j=PACK), rows.rearrange("(p j) c -> p j c", j=PACK))
+            raw[name, a, m] = dst
+
+        def load_st(m, dst):
+            nc.sync.dma_start(dst, st[m * P : (m + 1) * P, :])
+            state[m] = dst
+
+        def own(name):
+            return keep.tile([P, PIECE], F32, name=name, align_bytes=64)[:]
+
+        def load_scale_rows():
+            rows = x_scales.bitcast(I32).rearrange("a (g i) c -> i g a c", i=2)
+            for i in range(2):
+                nc.sync.dma_start(scale_table[i:P:PLANE, :].bitcast(I32), rows[i])
+
+        table = {}
+        load_scale_rows()
+        load_w("g", 0, 0, own("raw_g00"))
+        load_w("g", 1, 0, own("raw_g10"))
+        load_w("f", 0, 0, own("raw_f00"))
+        table[0] = load_words(0)
+        table[1] = load_words(1)
+        load_w("f", 1, 0, own("raw_f10"))
+        load_st(0, own("state0"))
+
+        warm = keep.tile([P, 1], F32, name="warm")
+        nc.vector.memset(warm[:], 0.0)
+        warm2 = keep.tile([P, 1], F32, name="warm2")
+        nc.scalar.activation(warm2[:], warm[:], TANH)
+
+        picked_bytes = keep.tile([P, S], U8, name="picked_bytes", tag="held", align_bytes=64)
+        nc.vector.tensor_copy(picked_bytes[:], scale_table[:].indirect(offsets[:]))
+        planes = keep.tile([P, S], U8, name="planes", align_bytes=64)
+        nc.vector.tensor_copy(planes[:].bitcast(I32), picked_bytes[:].bitcast(I32))
+        for a in range(PASSES):
+            for i in range(2):
+                r = PLANE * a + i
+                nc.scalar.dma_start(planes[r + 2 : P : 32, :].bitcast(I32), picked_bytes[r + 16 : P : 32, :].bitcast(I32))
+
+        late = keep.tile([P, 5 * PIECE], F32, name="late", tag="held", align_bytes=64)
+        for n, item in enumerate(["g01","g11","f01","f11","s1"]):
+            dst = late[:, n * PIECE : (n + 1) * PIECE]
+            if item[0] == "s":
+                load_st(int(item[1]), dst)
+            else:
+                load_w(item[0], int(item[1]), int(item[2]), dst)
+
+        woven = {}
+        quantized = {}
+        picked = {}
+        acc = {}
+        act = {}
+        diff = {}
+        gated = {}
+
+        def weave(name, a, m, eng):
+            t = keep.tile([P, P, PACK], BF16, name="woven_%s%d%d" % (name, a, m), align_bytes=64)
+            dst = t[:].rearrange("p (c i) t -> p c t i", i=4)
+            src = raw[name, a, m].rearrange("p (t c i) -> p c t i", t=PACK, i=4)
+            if eng == "s":
+                nc.scalar.copy(dst, src)
+            else:
+                nc.vector.tensor_copy(dst, src)
+            woven[name, a, m] = t
+
+        def quantize(name, a, m):
+            codes = keep.tile([P, P], U32, name="codes_%s%d%d" % (name, a, m), align_bytes=64)
+            scales = keep.tile([P, P], U8, name="scales_%s%d%d" % (name, a, m), align_bytes=64)
+            nc.vector.quantize_mx(out=codes[:].bitcast(FP8X4), scales=scales[:], in_=woven[name, a, m][:].rearrange("p c t -> p (c t)"))
+            quantized[name, a, m] = (codes, scales)
+
+        def gather_words(a):
+            t = keep.tile([P, S], U32, name="picked%d" % a, align_bytes=64)
+            nc.vector.tensor_copy(t[:], table[a][:].indirect(offsets[:]))
+            picked[a] = t
+
+        def product(name, a, m):
+            codes, scales = quantized[name, a, m]
+            for h in range(2):
+                if a == 0:
+                    acc[name, m, h] = psum.tile([P, HALF], F32, name="acc_%s%d%d" % (name, m, h))
+                cols = slice(h * HALF, (h + 1) * HALF)
+                nc.tensor.matmul_mx(
+                    out=acc[name, m, h][:],
+                    lhsT=codes[:].bitcast(FP8X4),
+                    lhsT_scale=scales[:],
+                    rhs=picked[a][:, cols].bitcast(FP8X4),
+                    rhs_scale=planes[PLANE * a : P, cols],
+                    start=(a == 0),
+                    stop=(a == PASSES - 1),
+                )
+
+        def squash(name, m):
+            for h in range(2):
+                t = keep.tile([P, HALF], F32, name="act_%s%d%d" % (name, m, h), align_bytes=64)
+                nc.scalar.activation(t[:], acc[name, m, h][:], TANH, scale=(1.0 if name == "g" else 0.5))
+                act[name, m, h] = t
+
+        def subtract(m):
+            for h in range(2):
+                t = keep.tile([P, HALF], F32, name="diff%d%d" % (m, h), align_bytes=64)
+                nc.vector.tensor_tensor(t[:], act["g", m, h][:], state[m][:, h * HALF : (h + 1) * HALF], SUB)
+                diff[m, h] = t
+
+        def gate(m):
+            for h in range(2):
+                t = keep.tile([P, HALF], F32, name="gated%d%d" % (m, h), align_bytes=64)
+                nc.vector.scalar_tensor_tensor(t[:], act["f", m, h][:], 1.0, diff[m, h][:], ADD, MULT)
+                gated[m, h] = t
+
+        def finish(m):
+            for h in range(2):
+                cols = slice(h * HALF, (h + 1) * HALF)
+                t = keep.tile([P, HALF], F32, name="new%d%d" % (m, h), align_bytes=64)
+                nc.vector.scalar_tensor_tensor(t[:], gated[m, h][:], 0.5, state[m][:, cols], MULT, ADD)
+                nc.sync.dma_start(out[m * P : (m + 1) * P, cols], t[:])
+
+        weave("g", 0, 0, "s")
+        weave("g", 1, 0, "s")
+        weave("f", 0, 0, "s")
+        quantize("g", 0, 0)
+        quantize("g", 1, 0)
+        quantize("f", 0, 0)
+        gather_words(0)
+        product("g", 0, 0)
+        product("f", 0, 0)
+        gather_words(1)
+        product("g", 1, 0)
+        weave("f", 1, 0, "s")
+        quantize("f", 1, 0)
+        product("f", 1, 0)
+        squash("g", 0)
+        squash("f", 0)
+        weave("g", 0, 1, "v")
+        quantize("g", 0, 1)
+        weave("g", 1, 1, "s")
+        quantize("g", 1, 1)
+        weave("f", 0, 1, "s")
+        quantize("f", 0, 1)
+        weave("f", 1, 1, "v")
+        quantize("f", 1, 1)
+        product("g", 0, 1)
+        product("g", 1, 1)
+        squash("g", 1)
+        product("f", 0, 1)
+        product("f", 1, 1)
+        squash("f", 1)
+        subtract(0)
+        gate(0)
+        finish(0)
+        subtract(1)
+        gate(1)
+        finish(1)

@@ -23,7 +23,6 @@ K_PASS = P * PACK
 PASSES = K // K_PASS
 HALF = S // 2
 PLANE = 8
-PIECE = PACK * P
 
 
 def tile_picked_phcell_none_p_kernel(tc, x_words, x_scales, w1, w2, st, offs, out):
@@ -33,173 +32,140 @@ def tile_picked_phcell_none_p_kernel(tc, x_words, x_scales, w1, w2, st, offs, ou
         keep = ctx.enter_context(tc.tile_pool(name="keep", bufs=1))
         psum = ctx.enter_context(tc.psum_pool(name="psum", bufs=1))
 
-        scale_table = keep.tile([P, T], U8, name="scale_table", align_bytes=64)
+        def tile(shape, dtype, name, tag=None):
+            return keep.tile(shape, dtype, name=name, tag=tag or name, align_bytes=64)
+
+        scale_table = tile([P, T], U8, "scale_table")
         nc.vector.memset(scale_table[:, : 3 * T // 4].bitcast(I32), 0)
         nc.gpsimd.memset(scale_table[:, 3 * T // 4 :].bitcast(I32), 0)
 
         offsets = keep.tile([P, S // 16], U16, name="offsets")
         nc.sync.dma_start(offsets[:], offs)
 
-        def load_words(a):
-            t = keep.tile([P, T], U32, name="word_table%d" % a, align_bytes=64)
-            nc.sync.dma_start(t[:].bitcast(I32), x_words[a].rearrange("p c r -> p (c r)").bitcast(I32))
-            return t
+        rows = x_scales.bitcast(I32).rearrange("a (g i) c -> i g a c", i=2)
+        for i in range(2):
+            nc.sync.dma_start(scale_table[i:P:PLANE, :].bitcast(I32), rows[i])
 
-        raw = {}
-        state = {}
+        table, raw, state, woven, quantized, picked, acc, act, diff, gated = {}, {}, {}, {}, {}, {}, {}, {}, {}, {}
 
-        def load_w(name, a, m, dst):
-            rows = weights[name][a * K_PASS : (a + 1) * K_PASS, m * P : (m + 1) * P]
-            nc.sync.dma_start(dst.rearrange("p (j c) -> p j c", j=PACK), rows.rearrange("(p j) c -> p j c", j=PACK))
-            raw[name, a, m] = dst
+        def load_words(a, tag=None):
+            table[a] = tile([P, T], U32, "word_table%d" % a, tag)
+            nc.sync.dma_start(table[a][:].bitcast(I32), x_words[a].rearrange("p c r -> p (c r)").bitcast(I32))
+
+        def load_w(name, a, c0, c1, parts=1, dst=None):
+            if dst is None:
+                dst = tile([P, PACK * (c1 - c0)], F32, "raw_%s%d_%d" % (name, a, c0))[:]
+            src = weights[name][a * K_PASS : (a + 1) * K_PASS, c0:c1].rearrange("(p j) c -> p j c", j=PACK)
+            step = PACK // parts
+            for j in range(0, PACK, step):
+                nc.sync.dma_start(dst.rearrange("p (j c) -> p j c", j=PACK)[:, j : j + step, :], src[:, j : j + step, :])
+            raw[name, a, c0] = dst
 
         def load_st(m, dst):
             nc.sync.dma_start(dst, st[m * P : (m + 1) * P, :])
             state[m] = dst
 
-        def own(name):
-            return keep.tile([P, PIECE], F32, name=name, align_bytes=64)[:]
-
-        def load_scale_rows():
-            rows = x_scales.bitcast(I32).rearrange("a (g i) c -> i g a c", i=2)
-            for i in range(2):
-                nc.sync.dma_start(scale_table[i:P:PLANE, :].bitcast(I32), rows[i])
-
-        table = {}
-        load_scale_rows()
-        load_w("g", 0, 0, own("raw_g00"))
-        load_w("g", 1, 0, own("raw_g10"))
-        load_w("f", 0, 0, own("raw_f00"))
-        table[0] = load_words(0)
-        table[1] = load_words(1)
-        load_w("f", 1, 0, own("raw_f10"))
-        load_st(0, own("state0"))
-
-        warm = keep.tile([P, 1], F32, name="warm")
-        nc.vector.memset(warm[:], 0.0)
-        warm2 = keep.tile([P, 1], F32, name="warm2")
-        nc.scalar.activation(warm2[:], warm[:], TANH)
-
-        picked_bytes = keep.tile([P, S], U8, name="picked_bytes", tag="held", align_bytes=64)
-        nc.vector.tensor_copy(picked_bytes[:], scale_table[:].indirect(offsets[:]))
-        planes = keep.tile([P, S], U8, name="planes", align_bytes=64)
-        nc.vector.tensor_copy(planes[:].bitcast(I32), picked_bytes[:].bitcast(I32))
-        for a in range(PASSES):
-            for i in range(2):
-                r = PLANE * a + i
-                nc.scalar.dma_start(planes[r + 2 : P : 32, :].bitcast(I32), picked_bytes[r + 16 : P : 32, :].bitcast(I32))
-
-        late = keep.tile([P, 5 * PIECE], F32, name="late", tag="held", align_bytes=64)
-        for n, item in enumerate(["g01","g11","f01","f11","s1"]):
-            dst = late[:, n * PIECE : (n + 1) * PIECE]
-            if item[0] == "s":
-                load_st(int(item[1]), dst)
-            else:
-                load_w(item[0], int(item[1]), int(item[2]), dst)
-
-        woven = {}
-        quantized = {}
-        picked = {}
-        acc = {}
-        act = {}
-        diff = {}
-        gated = {}
-
-        def weave(name, a, m, eng):
-            t = keep.tile([P, P, PACK], BF16, name="woven_%s%d%d" % (name, a, m), align_bytes=64)
+        def weave(name, a, c0, eng):
+            width = raw[name, a, c0].shape[1] // PACK
+            t = tile([P, width, PACK], BF16, "woven_%s%d_%d" % (name, a, c0))
             dst = t[:].rearrange("p (c i) t -> p c t i", i=4)
-            src = raw[name, a, m].rearrange("p (t c i) -> p c t i", t=PACK, i=4)
+            src = raw[name, a, c0].rearrange("p (t c i) -> p c t i", t=PACK, i=4)
             if eng == "s":
                 nc.scalar.copy(dst, src)
             else:
                 nc.vector.tensor_copy(dst, src)
-            woven[name, a, m] = t
+            woven[name, a, c0] = t
 
-        def quantize(name, a, m):
-            codes = keep.tile([P, P], U32, name="codes_%s%d%d" % (name, a, m), align_bytes=64)
-            scales = keep.tile([P, P], U8, name="scales_%s%d%d" % (name, a, m), align_bytes=64)
-            nc.vector.quantize_mx(out=codes[:].bitcast(FP8X4), scales=scales[:], in_=woven[name, a, m][:].rearrange("p c t -> p (c t)"))
-            quantized[name, a, m] = (codes, scales)
+        def quantize(name, a, c0):
+            width = woven[name, a, c0].shape[1]
+            codes = tile([P, width], U32, "codes_%s%d_%d" % (name, a, c0))
+            scales = tile([P, width], U8, "scales_%s%d_%d" % (name, a, c0))
+            nc.vector.quantize_mx(out=codes[:].bitcast(FP8X4), scales=scales[:], in_=woven[name, a, c0][:].rearrange("p c t -> p (c t)"))
+            for c in range(0, width, P):
+                quantized[name, a, (c0 + c) // P] = (codes[:, c : c + P], scales[:, c : c + P])
 
-        def gather_words(a):
-            t = keep.tile([P, S], U32, name="picked%d" % a, align_bytes=64)
-            nc.vector.tensor_copy(t[:], table[a][:].indirect(offsets[:]))
-            picked[a] = t
+        def gather_words(a, h):
+            picked[a, h] = tile([P, HALF], U32, "picked%d%d" % (a, h))
+            nc.vector.tensor_copy(picked[a, h][:], table[a][:].indirect(offsets[:, h * HALF // 16 : (h + 1) * HALF // 16]))
 
-        def product(name, a, m):
+        def product(name, a, m, h):
             codes, scales = quantized[name, a, m]
-            for h in range(2):
-                if a == 0:
-                    acc[name, m, h] = psum.tile([P, HALF], F32, name="acc_%s%d%d" % (name, m, h))
-                cols = slice(h * HALF, (h + 1) * HALF)
-                nc.tensor.matmul_mx(
-                    out=acc[name, m, h][:],
-                    lhsT=codes[:].bitcast(FP8X4),
-                    lhsT_scale=scales[:],
-                    rhs=picked[a][:, cols].bitcast(FP8X4),
-                    rhs_scale=planes[PLANE * a : P, cols],
-                    start=(a == 0),
-                    stop=(a == PASSES - 1),
-                )
+            if a == 0:
+                acc[name, m, h] = psum.tile([P, HALF], F32, name="acc_%s%d%d" % (name, m, h))
+            nc.tensor.matmul_mx(
+                out=acc[name, m, h][:],
+                lhsT=codes.bitcast(FP8X4),
+                lhsT_scale=scales,
+                rhs=picked[a, h][:].bitcast(FP8X4),
+                rhs_scale=planes[PLANE * a : P, h * HALF : (h + 1) * HALF],
+                start=(a == 0),
+                stop=(a == PASSES - 1),
+            )
 
-        def squash(name, m):
-            for h in range(2):
-                t = keep.tile([P, HALF], F32, name="act_%s%d%d" % (name, m, h), align_bytes=64)
-                nc.scalar.activation(t[:], acc[name, m, h][:], TANH, scale=(1.0 if name == "g" else 0.5))
-                act[name, m, h] = t
+        def squash(name, m, h):
+            act[name, m, h] = tile([P, HALF], F32, "act_%s%d%d" % (name, m, h))
+            nc.scalar.activation(act[name, m, h][:], acc[name, m, h][:], TANH, scale=(1.0 if name == "g" else 0.5))
 
-        def subtract(m):
-            for h in range(2):
-                t = keep.tile([P, HALF], F32, name="diff%d%d" % (m, h), align_bytes=64)
-                nc.vector.tensor_tensor(t[:], act["g", m, h][:], state[m][:, h * HALF : (h + 1) * HALF], SUB)
-                diff[m, h] = t
+        def subtract(m, h):
+            diff[m, h] = tile([P, HALF], F32, "diff%d%d" % (m, h))
+            nc.vector.tensor_tensor(diff[m, h][:], act["g", m, h][:], state[m][:, h * HALF : (h + 1) * HALF], SUB)
 
-        def gate(m):
-            for h in range(2):
-                t = keep.tile([P, HALF], F32, name="gated%d%d" % (m, h), align_bytes=64)
-                nc.vector.scalar_tensor_tensor(t[:], act["f", m, h][:], 1.0, diff[m, h][:], ADD, MULT)
-                gated[m, h] = t
+        def gate(m, h):
+            gated[m, h] = tile([P, HALF], F32, "gated%d%d" % (m, h))
+            nc.vector.scalar_tensor_tensor(gated[m, h][:], act["f", m, h][:], 1.0, diff[m, h][:], ADD, MULT)
 
-        def finish(m):
-            for h in range(2):
-                cols = slice(h * HALF, (h + 1) * HALF)
-                t = keep.tile([P, HALF], F32, name="new%d%d" % (m, h), align_bytes=64)
-                nc.vector.scalar_tensor_tensor(t[:], gated[m, h][:], 0.5, state[m][:, cols], MULT, ADD)
-                nc.sync.dma_start(out[m * P : (m + 1) * P, cols], t[:])
+        def finish(m, h):
+            cols = slice(h * HALF, (h + 1) * HALF)
+            t = tile([P, HALF], F32, "new%d%d" % (m, h))
+            nc.vector.scalar_tensor_tensor(t[:], gated[m, h][:], 0.5, state[m][:, cols], MULT, ADD)
+            nc.sync.dma_start(out[m * P : (m + 1) * P, cols], t[:])
 
-        weave("g", 0, 0, "s")
-        weave("g", 1, 0, "s")
-        weave("f", 0, 0, "s")
-        quantize("g", 0, 0)
-        quantize("g", 1, 0)
-        quantize("f", 0, 0)
-        gather_words(0)
-        product("g", 0, 0)
-        product("f", 0, 0)
-        gather_words(1)
-        product("g", 1, 0)
-        weave("f", 1, 0, "s")
-        quantize("f", 1, 0)
-        product("f", 1, 0)
-        squash("g", 0)
-        squash("f", 0)
-        weave("g", 0, 1, "v")
-        quantize("g", 0, 1)
-        weave("g", 1, 1, "s")
-        quantize("g", 1, 1)
-        weave("f", 0, 1, "s")
-        quantize("f", 0, 1)
-        weave("f", 1, 1, "v")
-        quantize("f", 1, 1)
-        product("g", 0, 1)
-        product("g", 1, 1)
-        squash("g", 1)
-        product("f", 0, 1)
-        product("f", 1, 1)
-        squash("f", 1)
-        subtract(0)
-        gate(0)
-        finish(0)
-        subtract(1)
-        gate(1)
-        finish(1)
+        load_w("g", 0, 0, N, parts=4)
+        load_w("f", 0, 0, N)
+        load_w("g", 1, 0, N)
+        load_w("f", 1, 0, N)
+        load_words(0)
+
+        warm = tile([P, 1], F32, "warm")
+        nc.vector.memset(warm[:], 0.0)
+        warm2 = tile([P, 1], F32, "warm2")
+        nc.scalar.activation(warm2[:], warm[:], TANH)
+
+        picked_bytes = tile([P, S], U8, "picked_bytes")
+        nc.vector.tensor_copy(picked_bytes[:], scale_table[:].indirect(offsets[:]))
+        planes = tile([P, S], U8, "planes")
+        nc.vector.tensor_copy(planes[:].bitcast(I32), picked_bytes[:].bitcast(I32))
+        for a in range(PASSES):
+            for i in range(2):
+                r = PLANE * a + i
+                nc.sync.dma_start(planes[r + 2 : P : 32, :].bitcast(I32), planes[r + 16 : P : 32, :].bitcast(I32))
+
+        load_words(1, "picked_bytes")
+        for name, a in (("g", 0), ("f", 0), ("g", 1), ("f", 1)):
+            weave(name, a, 0, "s")
+            quantize(name, a, 0)
+        both = tile([P, 2 * S], F32, "state", "raw_g1_0")
+        for m in range(2):
+            load_st(m, both[:, m * S : (m + 1) * S])
+        for a in range(PASSES):
+            for h in range(2):
+                gather_words(a, h)
+                for m in range(2):
+                    for name in ("g", "f"):
+                        product(name, a, m, h)
+        for h in range(2):
+            for m in range(2):
+                squash("g", m, h)
+                squash("f", m, h)
+        subtract(0, 0)
+        gate(0, 0)
+        subtract(1, 0)
+        finish(0, 0)
+        gate(1, 0)
+        subtract(0, 1)
+        finish(1, 0)
+        gate(0, 1)
+        subtract(1, 1)
+        finish(0, 1)
+        gate(1, 1)
+        finish(1, 1)

@@ -65,15 +65,16 @@ def tile_picked_phcell_none_p_kernel(tc, x_words, x_scales, w1, w2, st, offs, ou
             nc.sync.dma_start(dst, st[m * P : (m + 1) * P, :])
             state[m] = dst
 
-        def weave(name, a, c0, eng):
+        def weave(name, a, c0, on_scalar):
             width = raw[name, a, c0].shape[1] // PACK
             t = tile([P, width, PACK], BF16, "woven_%s%d_%d" % (name, a, c0))
             dst = t[:].rearrange("p (c i) t -> p c t i", i=4)
             src = raw[name, a, c0].rearrange("p (t c i) -> p c t i", t=PACK, i=4)
-            if eng == "s":
-                nc.scalar.copy(dst, src)
-            else:
-                nc.vector.tensor_copy(dst, src)
+            cut = on_scalar // 4
+            if cut > 0:
+                nc.scalar.copy(dst[:, :cut], src[:, :cut])
+            if on_scalar < width:
+                nc.vector.tensor_copy(dst[:, cut:], src[:, cut:])
             woven[name, a, c0] = t
 
         def quantize(name, a, c0):
@@ -103,28 +104,28 @@ def tile_picked_phcell_none_p_kernel(tc, x_words, x_scales, w1, w2, st, offs, ou
             )
 
         def squash(name, m, h):
-            act[name, m, h] = tile([P, HALF], F32, "act_%s%d%d" % (name, m, h))
-            nc.scalar.activation(act[name, m, h][:], acc[name, m, h][:], TANH, scale=(1.0 if name == "g" else 0.5))
+            if m == 0:
+                act[name, h] = tile([P, 2, HALF], F32, "act_%s%d" % (name, h))
+            nc.scalar.activation(act[name, h][:, m, :], acc[name, m, h][:], TANH, scale=(1.0 if name == "g" else 0.5))
 
-        def subtract(m, h):
-            diff[m, h] = tile([P, HALF], F32, "diff%d%d" % (m, h))
-            nc.vector.tensor_tensor(diff[m, h][:], act["g", m, h][:], state[m][:, h * HALF : (h + 1) * HALF], SUB)
+        def subtract(h):
+            diff[h] = tile([P, 2, HALF], F32, "diff%d" % h, "woven_f1_%d" % (P * (1 - h)))
+            nc.vector.tensor_tensor(diff[h][:], act["g", h][:], state[0][:, :, h * HALF : (h + 1) * HALF], SUB)
 
-        def gate(m, h):
-            gated[m, h] = tile([P, HALF], F32, "gated%d%d" % (m, h))
-            nc.vector.scalar_tensor_tensor(gated[m, h][:], act["f", m, h][:], 1.0, diff[m, h][:], ADD, MULT)
+        def gate(h):
+            gated[h] = tile([P, 2, HALF], F32, "gated%d" % h)
+            nc.vector.scalar_tensor_tensor(gated[h][:], act["f", h][:], 1.0, diff[h][:], ADD, MULT)
 
-        def finish(m, h):
+        def finish(h, m0, m1):
             cols = slice(h * HALF, (h + 1) * HALF)
-            t = tile([P, HALF], F32, "new%d%d" % (m, h))
-            nc.vector.scalar_tensor_tensor(t[:], gated[m, h][:], 0.5, state[m][:, cols], MULT, ADD)
-            nc.sync.dma_start(out[m * P : (m + 1) * P, cols], t[:])
+            t = tile([P, m1 - m0, HALF], F32, "new%d%d" % (h, m0))
+            nc.vector.scalar_tensor_tensor(t[:], gated[h][:, m0:m1, :], 0.5, state[0][:, m0:m1, cols], MULT, ADD)
+            nc.sync.dma_start(out.rearrange("(m p) s -> p m s", p=P)[:, m0:m1, cols], t[:])
 
         load_w("g", 0, 0, N, parts=4)
         load_w("f", 0, 0, N)
-        load_w("g", 1, 0, N)
-        load_w("f", 1, 0, N)
         load_words(0)
+        load_w("g", 1, 0, N)
 
         warm = tile([P, 1], F32, "warm")
         nc.vector.memset(warm[:], 0.0)
@@ -141,31 +142,42 @@ def tile_picked_phcell_none_p_kernel(tc, x_words, x_scales, w1, w2, st, offs, ou
                 nc.sync.dma_start(planes[r + 2 : P : 32, :].bitcast(I32), planes[r + 16 : P : 32, :].bitcast(I32))
 
         load_words(1, "picked_bytes")
-        for name, a in (("g", 0), ("f", 0), ("g", 1), ("f", 1)):
-            weave(name, a, 0, "s")
-            quantize(name, a, 0)
-        both = tile([P, 2 * S], F32, "state", "raw_g1_0")
-        for m in range(2):
-            load_st(m, both[:, m * S : (m + 1) * S])
-        for a in range(PASSES):
-            for h in range(2):
-                gather_words(a, h)
+        weave("g", 0, 0, N)
+        quantize("g", 0, 0)
+        weave("f", 0, 0, N)
+        quantize("f", 0, 0)
+        late = tile([P, PACK * N + 2 * S], F32, "late", "raw_f0_0")
+        load_w("f", 1, 0, N, dst=late[:, : PACK * N])
+        state[0] = late[:, PACK * N :].rearrange("p (m s) -> p m s", m=2)
+        nc.sync.dma_start(state[0], st.rearrange("(m p) s -> p m s", p=P))
+        for h in range(2):
+            gather_words(0, h)
+            for name in ("g", "f"):
                 for m in range(2):
-                    for name in ("g", "f"):
-                        product(name, a, m, h)
+                    product(name, 0, m, h)
+        weave("g", 1, 0, N)
+        quantize("g", 1, 0)
+        for h in range(2):
+            gather_words(1, h)
+            for m in range(2):
+                product("g", 1, m, h)
+        whole = raw["f", 1, 0].rearrange("p (t c i) -> p c t i", t=PACK, i=4)
+        for m in range(2):
+            woven["f", 1, m * P] = tile([P, P, PACK], BF16, "woven_f1_%d" % (m * P))
+            nc.vector.tensor_copy(woven["f", 1, m * P][:].rearrange("p (c i) t -> p c t i", i=4), whole[:, m * P // 4 : (m + 1) * P // 4])
+        for m in range(2):
+            quantize("f", 1, m * P)
         for h in range(2):
             for m in range(2):
                 squash("g", m, h)
+        for h in range(2):
+            for m in range(2):
+                product("f", 1, m, h)
                 squash("f", m, h)
-        subtract(0, 0)
-        gate(0, 0)
-        subtract(1, 0)
-        finish(0, 0)
-        gate(1, 0)
-        subtract(0, 1)
-        finish(1, 0)
-        gate(0, 1)
-        subtract(1, 1)
-        finish(0, 1)
-        gate(1, 1)
-        finish(1, 1)
+        subtract(0)
+        subtract(1)
+        gate(0)
+        gate(1)
+        finish(0, 0, 2)
+        finish(1, 0, 1)
+        finish(1, 1, 2)

@@ -21,8 +21,15 @@ P = 128
 PACK = 4
 K_PASS = P * PACK
 PASSES = K // K_PASS
-HALF = S // 2
-PLANE = 8
+ROW_TILES = N // P
+HALVES = 2
+HALF = S // HALVES
+GROUP = 16
+QUADRANT = 32
+RUN_ROWS = 2
+PLANE_STEP = 8
+NEAR = 4
+CLEAR_SPLIT = 3 * T // 4
 
 
 def tile_picked_phcell_none_p_kernel(tc, x_words, x_scales, w1, w2, st, offs, out):
@@ -32,62 +39,51 @@ def tile_picked_phcell_none_p_kernel(tc, x_words, x_scales, w1, w2, st, offs, ou
         keep = ctx.enter_context(tc.tile_pool(name="keep", bufs=1))
         psum = ctx.enter_context(tc.psum_pool(name="psum", bufs=1))
 
-        def tile(shape, dtype, name, tag=None):
-            return keep.tile(shape, dtype, name=name, tag=tag or name, align_bytes=64)
+        def tile(shape, dtype, name, reuse=None):
+            return keep.tile(shape, dtype, name=name, tag=reuse or name, align_bytes=64)
 
         scale_table = tile([P, T], U8, "scale_table")
-        nc.vector.memset(scale_table[:, : 3 * T // 4].bitcast(I32), 0)
-        nc.gpsimd.memset(scale_table[:, 3 * T // 4 :].bitcast(I32), 0)
+        nc.vector.memset(scale_table[:, :CLEAR_SPLIT].bitcast(I32), 0)
+        nc.gpsimd.memset(scale_table[:, CLEAR_SPLIT:].bitcast(I32), 0)
 
-        offsets = keep.tile([P, S // 16], U16, name="offsets")
+        offsets = keep.tile([P, S // GROUP], U16, name="offsets")
         nc.sync.dma_start(offsets[:], offs)
 
-        rows = x_scales.bitcast(I32).rearrange("a (g i) c -> i g a c", i=2)
-        for i in range(2):
-            nc.sync.dma_start(scale_table[i:P:PLANE, :].bitcast(I32), rows[i])
+        scale_rows = x_scales.bitcast(I32).rearrange("a (r i) c -> i r a c", i=RUN_ROWS)
+        for i in range(RUN_ROWS):
+            nc.sync.dma_start(scale_table[i:P:PLANE_STEP, :].bitcast(I32), scale_rows[i])
 
-        table, raw, state, woven, quantized, picked, acc, act, diff, gated = {}, {}, {}, {}, {}, {}, {}, {}, {}, {}
+        word_table, raw, quantized, picked, acc, act, diff, gated = {}, {}, {}, {}, {}, {}, {}, {}
 
-        def load_words(a, tag=None):
-            table[a] = tile([P, T], U32, "word_table%d" % a, tag)
-            nc.sync.dma_start(table[a][:].bitcast(I32), x_words[a].rearrange("p c r -> p (c r)").bitcast(I32))
+        def load_words(a, reuse=None):
+            word_table[a] = tile([P, T], U32, "word_table%d" % a, reuse)
+            nc.sync.dma_start(word_table[a][:].bitcast(I32), x_words[a].rearrange("p c t -> p (c t)").bitcast(I32))
 
-        def load_w(name, a, c0, c1, parts=1, dst=None):
-            if dst is None:
-                dst = tile([P, PACK * (c1 - c0)], F32, "raw_%s%d_%d" % (name, a, c0))[:]
-            src = weights[name][a * K_PASS : (a + 1) * K_PASS, c0:c1].rearrange("(p j) c -> p j c", j=PACK)
+        def load_weights(name, a, dst, parts=1):
+            src = weights[name][a * K_PASS : (a + 1) * K_PASS, :].rearrange("(p t) c -> p t c", t=PACK)
             step = PACK // parts
-            for j in range(0, PACK, step):
-                nc.sync.dma_start(dst.rearrange("p (j c) -> p j c", j=PACK)[:, j : j + step, :], src[:, j : j + step, :])
-            raw[name, a, c0] = dst
+            for t in range(0, PACK, step):
+                nc.sync.dma_start(dst.rearrange("p (t c) -> p t c", t=PACK)[:, t : t + step, :], src[:, t : t + step, :])
+            raw[name, a] = dst
 
-        def load_st(m, dst):
-            nc.sync.dma_start(dst, st[m * P : (m + 1) * P, :])
-            state[m] = dst
+        def weave(copy, name, a, m0, m1):
+            woven = tile([P, (m1 - m0) * P, PACK], BF16, "woven_%s%d_%d" % (name, a, m0))
+            src = raw[name, a].rearrange("p (t c i) -> p c t i", t=PACK, i=NEAR)
+            copy(woven[:].rearrange("p (c i) t -> p c t i", i=NEAR), src[:, m0 * P // NEAR : m1 * P // NEAR])
+            return woven
 
-        def weave(name, a, c0, on_scalar):
-            width = raw[name, a, c0].shape[1] // PACK
-            t = tile([P, width, PACK], BF16, "woven_%s%d_%d" % (name, a, c0))
-            dst = t[:].rearrange("p (c i) t -> p c t i", i=4)
-            src = raw[name, a, c0].rearrange("p (t c i) -> p c t i", t=PACK, i=4)
-            cut = on_scalar // 4
-            if cut > 0:
-                nc.scalar.copy(dst[:, :cut], src[:, :cut])
-            if on_scalar < width:
-                nc.vector.tensor_copy(dst[:, cut:], src[:, cut:])
-            woven[name, a, c0] = t
-
-        def quantize(name, a, c0):
-            width = woven[name, a, c0].shape[1]
-            codes = tile([P, width], U32, "codes_%s%d_%d" % (name, a, c0))
-            scales = tile([P, width], U8, "scales_%s%d_%d" % (name, a, c0))
-            nc.vector.quantize_mx(out=codes[:].bitcast(FP8X4), scales=scales[:], in_=woven[name, a, c0][:].rearrange("p c t -> p (c t)"))
+        def quantize(woven, name, a, m0):
+            width = woven.shape[1]
+            codes = tile([P, width], U32, "codes_%s%d_%d" % (name, a, m0))
+            scales = tile([P, width], U8, "scales_%s%d_%d" % (name, a, m0))
+            nc.vector.quantize_mx(out=codes[:].bitcast(FP8X4), scales=scales[:], in_=woven[:].rearrange("p c t -> p (c t)"))
             for c in range(0, width, P):
-                quantized[name, a, (c0 + c) // P] = (codes[:, c : c + P], scales[:, c : c + P])
+                quantized[name, a, m0 + c // P] = (codes[:, c : c + P], scales[:, c : c + P])
 
         def gather_words(a, h):
             picked[a, h] = tile([P, HALF], U32, "picked%d%d" % (a, h))
-            nc.vector.tensor_copy(picked[a, h][:], table[a][:].indirect(offsets[:, h * HALF // 16 : (h + 1) * HALF // 16]))
+            entries = offsets[:, h * HALF // GROUP : (h + 1) * HALF // GROUP]
+            nc.vector.tensor_copy(picked[a, h][:], word_table[a][:].indirect(entries))
 
         def product(name, a, m, h):
             codes, scales = quantized[name, a, m]
@@ -98,86 +94,83 @@ def tile_picked_phcell_none_p_kernel(tc, x_words, x_scales, w1, w2, st, offs, ou
                 lhsT=codes.bitcast(FP8X4),
                 lhsT_scale=scales,
                 rhs=picked[a, h][:].bitcast(FP8X4),
-                rhs_scale=planes[PLANE * a : P, h * HALF : (h + 1) * HALF],
+                rhs_scale=planes[PLANE_STEP * a : P, h * HALF : (h + 1) * HALF],
                 start=(a == 0),
                 stop=(a == PASSES - 1),
             )
 
         def squash(name, m, h):
             if m == 0:
-                act[name, h] = tile([P, 2, HALF], F32, "act_%s%d" % (name, h))
+                act[name, h] = tile([P, ROW_TILES, HALF], F32, "act_%s%d" % (name, h))
             nc.scalar.activation(act[name, h][:, m, :], acc[name, m, h][:], TANH, scale=(1.0 if name == "g" else 0.5))
 
-        def subtract(h):
-            diff[h] = tile([P, 2, HALF], F32, "diff%d" % h, "woven_f1_%d" % (P * (1 - h)))
-            nc.vector.tensor_tensor(diff[h][:], act["g", h][:], state[0][:, :, h * HALF : (h + 1) * HALF], SUB)
+        def subtract(h, reuse):
+            diff[h] = tile([P, ROW_TILES, HALF], F32, "diff%d" % h, reuse)
+            nc.vector.tensor_tensor(diff[h][:], act["g", h][:], state[:, :, h * HALF : (h + 1) * HALF], SUB)
 
-        def gate(h):
-            gated[h] = tile([P, 2, HALF], F32, "gated%d" % h)
-            nc.vector.scalar_tensor_tensor(gated[h][:], act["f", h][:], 1.0, diff[h][:], ADD, MULT)
+        def gate(h, m0, m1):
+            if m0 == 0:
+                gated[h] = tile([P, ROW_TILES, HALF], F32, "gated%d" % h)
+            nc.vector.scalar_tensor_tensor(gated[h][:, m0:m1, :], act["f", h][:, m0:m1, :], 1.0, diff[h][:, m0:m1, :], ADD, MULT)
 
         def finish(h, m0, m1):
             cols = slice(h * HALF, (h + 1) * HALF)
-            t = tile([P, m1 - m0, HALF], F32, "new%d%d" % (h, m0))
-            nc.vector.scalar_tensor_tensor(t[:], gated[h][:, m0:m1, :], 0.5, state[0][:, m0:m1, cols], MULT, ADD)
-            nc.sync.dma_start(out.rearrange("(m p) s -> p m s", p=P)[:, m0:m1, cols], t[:])
+            new = tile([P, m1 - m0, HALF], F32, "new%d%d" % (h, m0))
+            nc.vector.scalar_tensor_tensor(new[:], gated[h][:, m0:m1, :], 0.5, state[:, m0:m1, cols], MULT, ADD)
+            nc.sync.dma_start(out.rearrange("(m p) s -> p m s", p=P)[:, m0:m1, cols], new[:])
 
-        load_w("g", 0, 0, N, parts=4)
-        load_w("f", 0, 0, N)
+        load_weights("g", 0, tile([P, PACK * N], F32, "raw_g0")[:], parts=PACK)
+        load_weights("f", 0, tile([P, PACK * N], F32, "raw_f0")[:])
         load_words(0)
-        load_w("g", 1, 0, N)
-
-        warm = tile([P, 1], F32, "warm")
-        nc.vector.memset(warm[:], 0.0)
-        warm2 = tile([P, 1], F32, "warm2")
-        nc.scalar.activation(warm2[:], warm[:], TANH)
+        load_weights("g", 1, tile([P, PACK * N], F32, "raw_g1")[:])
 
         picked_bytes = tile([P, S], U8, "picked_bytes")
         nc.vector.tensor_copy(picked_bytes[:], scale_table[:].indirect(offsets[:]))
         planes = tile([P, S], U8, "planes")
         nc.vector.tensor_copy(planes[:].bitcast(I32), picked_bytes[:].bitcast(I32))
         for a in range(PASSES):
-            for i in range(2):
-                r = PLANE * a + i
-                nc.sync.dma_start(planes[r + 2 : P : 32, :].bitcast(I32), planes[r + 16 : P : 32, :].bitcast(I32))
+            for i in range(RUN_ROWS):
+                row = PLANE_STEP * a + i
+                nc.sync.dma_start(
+                    planes[row + RUN_ROWS : P : QUADRANT, :].bitcast(I32), planes[row + GROUP : P : QUADRANT, :].bitcast(I32)
+                )
 
-        load_words(1, "picked_bytes")
-        weave("g", 0, 0, N)
-        quantize("g", 0, 0)
-        weave("f", 0, 0, N)
-        quantize("f", 0, 0)
-        late = tile([P, PACK * N + 2 * S], F32, "late", "raw_f0_0")
-        load_w("f", 1, 0, N, dst=late[:, : PACK * N])
-        state[0] = late[:, PACK * N :].rearrange("p (m s) -> p m s", m=2)
-        nc.sync.dma_start(state[0], st.rearrange("(m p) s -> p m s", p=P))
-        for h in range(2):
+        load_words(1, reuse="picked_bytes")
+        quantize(weave(nc.scalar.copy, "g", 0, 0, ROW_TILES), "g", 0, 0)
+        last = tile([P, PACK * N + ROW_TILES * S], F32, "last", reuse="raw_g0")
+        load_weights("f", 1, last[:, : PACK * N])
+        state = last[:, PACK * N :].rearrange("p (m s) -> p m s", m=ROW_TILES)
+        nc.sync.dma_start(state, st.rearrange("(m p) s -> p m s", p=P))
+        quantize(weave(nc.scalar.copy, "f", 0, 0, ROW_TILES), "f", 0, 0)
+
+        for h in range(HALVES):
             gather_words(0, h)
             for name in ("g", "f"):
-                for m in range(2):
+                for m in range(ROW_TILES):
                     product(name, 0, m, h)
-        weave("g", 1, 0, N)
-        quantize("g", 1, 0)
-        for h in range(2):
+
+        quantize(weave(nc.scalar.copy, "g", 1, 0, ROW_TILES), "g", 1, 0)
+        for h in range(HALVES):
             gather_words(1, h)
-            for m in range(2):
+            for m in range(ROW_TILES):
                 product("g", 1, m, h)
-        whole = raw["f", 1, 0].rearrange("p (t c i) -> p c t i", t=PACK, i=4)
-        for m in range(2):
-            woven["f", 1, m * P] = tile([P, P, PACK], BF16, "woven_f1_%d" % (m * P))
-            nc.vector.tensor_copy(woven["f", 1, m * P][:].rearrange("p (c i) t -> p c t i", i=4), whole[:, m * P // 4 : (m + 1) * P // 4])
-        for m in range(2):
-            quantize("f", 1, m * P)
-        for h in range(2):
-            for m in range(2):
+
+        woven_last = [weave(nc.vector.tensor_copy, "f", 1, m, m + 1) for m in range(ROW_TILES)]
+        for m in range(ROW_TILES):
+            quantize(woven_last[m], "f", 1, m)
+        for h in range(HALVES):
+            for m in range(ROW_TILES):
                 squash("g", m, h)
-        for h in range(2):
-            for m in range(2):
+        for h in range(HALVES):
+            for m in range(ROW_TILES):
                 product("f", 1, m, h)
                 squash("f", m, h)
-        subtract(0)
-        subtract(1)
-        gate(0)
-        gate(1)
-        finish(0, 0, 2)
+
+        subtract(0, reuse="woven_f1_1")
+        subtract(1, reuse="woven_f1_0")
+        gate(0, 0, ROW_TILES)
+        gate(1, 0, 1)
+        finish(0, 0, ROW_TILES)
+        gate(1, 1, 2)
         finish(1, 0, 1)
         finish(1, 1, 2)

@@ -29,7 +29,6 @@ QUADRANT = 32
 RUN_ROWS = 2
 PLANE_STEP = 8
 NEAR = 4
-CLEAR_SPLIT = 3 * T // 4
 
 
 def tile_picked_phcell_none_p_kernel(tc, x_words, x_scales, w1, w2, st, offs, out):
@@ -43,8 +42,7 @@ def tile_picked_phcell_none_p_kernel(tc, x_words, x_scales, w1, w2, st, offs, ou
             return keep.tile(shape, dtype, name=name, tag=reuse or name, align_bytes=64)
 
         scale_table = tile([P, T], U8, "scale_table")
-        nc.vector.memset(scale_table[:, :CLEAR_SPLIT].bitcast(I32), 0)
-        nc.gpsimd.memset(scale_table[:, CLEAR_SPLIT:].bitcast(I32), 0)
+        nc.vector.memset(scale_table[:].bitcast(I32), 0)
 
         offsets = keep.tile([P, S // GROUP], U16, name="offsets")
         nc.sync.dma_start(offsets[:], offs)

from contextlib import ExitStack

import concourse.mybir as mybir

K, T, S, N = 1024, 2048, 512, 256
FLOPS = 2 * 2 * K * S * N

F32 = mybir.dt.float32
BF16 = mybir.dt.bfloat16
I32 = mybir.dt.int32
U32 = mybir.dt.uint32
U16 = mybir.dt.uint16
U8 = mybir.dt.uint8
FP8X4 = mybir.dt.float8_e4m3fn_x4
TANH = mybir.ActivationFunctionType.Tanh
ADD = mybir.AluOpType.add
SUB = mybir.AluOpType.subtract
MULT = mybir.AluOpType.mult

P = 128
PACK = 4
K_PASS = P * PACK
PASSES = K // K_PASS
ROW_TILES = N // P
HALVES = 2
HALF = S // HALVES
GROUP = 16
QUADRANT = 32
RUN_ROWS = 2
PLANE_STEP = 8
NEAR = 4


def tile_picked_phcell_none_p_kernel(tc, x_words, x_scales, w1, w2, st, offs, out):
    nc = tc.nc
    weights = {"f": w1, "g": w2}
    with ExitStack() as ctx:
        keep = ctx.enter_context(tc.tile_pool(name="keep", bufs=1))
        psum = ctx.enter_context(tc.psum_pool(name="psum", bufs=1))

        def tile(shape, dtype, name, reuse=None):
            return keep.tile(shape, dtype, name=name, tag=reuse or name, align_bytes=64)

        scale_table = tile([P, T], U8, "scale_table")
        nc.vector.memset(scale_table[:].bitcast(I32), 0)

        offsets = keep.tile([P, S // GROUP], U16, name="offsets")
        nc.sync.dma_start(offsets[:], offs)

        scale_rows = x_scales.bitcast(I32).rearrange("a (r i) c -> i r a c", i=RUN_ROWS)
        for i in range(RUN_ROWS):
            nc.sync.dma_start(scale_table[i:P:PLANE_STEP, :].bitcast(I32), scale_rows[i])

        word_table, raw, quantized, picked, acc, act, diff, gated = {}, {}, {}, {}, {}, {}, {}, {}

        def load_words(a, reuse=None):
            word_table[a] = tile([P, T], U32, "word_table%d" % a, reuse)
            nc.sync.dma_start(word_table[a][:].bitcast(I32), x_words[a].rearrange("p c t -> p (c t)").bitcast(I32))

        def load_weights(name, a, dst, parts=1):
            src = weights[name][a * K_PASS : (a + 1) * K_PASS, :].rearrange("(p t) c -> p t c", t=PACK)
            step = PACK // parts
            for t in range(0, PACK, step):
                nc.sync.dma_start(dst.rearrange("p (t c) -> p t c", t=PACK)[:, t : t + step, :], src[:, t : t + step, :])
            raw[name, a] = dst

        def weave(copy, name, a, m0, m1):
            woven = tile([P, (m1 - m0) * P, PACK], BF16, "woven_%s%d_%d" % (name, a, m0))
            src = raw[name, a].rearrange("p (t c i) -> p c t i", t=PACK, i=NEAR)
            copy(woven[:].rearrange("p (c i) t -> p c t i", i=NEAR), src[:, m0 * P // NEAR : m1 * P // NEAR])
            return woven

        def quantize(woven, name, a, m0):
            width = woven.shape[1]
            codes = tile([P, width], U32, "codes_%s%d_%d" % (name, a, m0))
            scales = tile([P, width], U8, "scales_%s%d_%d" % (name, a, m0))
            nc.vector.quantize_mx(out=codes[:].bitcast(FP8X4), scales=scales[:], in_=woven[:].rearrange("p c t -> p (c t)"))
            for c in range(0, width, P):
                quantized[name, a, m0 + c // P] = (codes[:, c : c + P], scales[:, c : c + P])

        def gather_words(a, h):
            picked[a, h] = tile([P, HALF], U32, "picked%d%d" % (a, h))
            entries = offsets[:, h * HALF // GROUP : (h + 1) * HALF // GROUP]
            nc.vector.tensor_copy(picked[a, h][:], word_table[a][:].indirect(entries))

        def product(name, a, m, h):
            codes, scales = quantized[name, a, m]
            if a == 0:
                acc[name, m, h] = psum.tile([P, HALF], F32, name="acc_%s%d%d" % (name, m, h))
            nc.tensor.matmul_mx(
                out=acc[name, m, h][:],
                lhsT=codes.bitcast(FP8X4),
                lhsT_scale=scales,
                rhs=picked[a, h][:].bitcast(FP8X4),
                rhs_scale=planes[PLANE_STEP * a : P, h * HALF : (h + 1) * HALF],
                start=(a == 0),
                stop=(a == PASSES - 1),
            )

        def squash(name, m, h):
            if m == 0:
                act[name, h] = tile([P, ROW_TILES, HALF], F32, "act_%s%d" % (name, h))
            nc.scalar.activation(act[name, h][:, m, :], acc[name, m, h][:], TANH, scale=(1.0 if name == "g" else 0.5))

        def subtract(h, reuse):
            diff[h] = tile([P, ROW_TILES, HALF], F32, "diff%d" % h, reuse)
            nc.vector.tensor_tensor(diff[h][:], act["g", h][:], state[:, :, h * HALF : (h + 1) * HALF], SUB)

        def gate(h, m0, m1):
            if m0 == 0:
                gated[h] = tile([P, ROW_TILES, HALF], F32, "gated%d" % h)
            nc.vector.scalar_tensor_tensor(gated[h][:, m0:m1, :], act["f", h][:, m0:m1, :], 1.0, diff[h][:, m0:m1, :], ADD, MULT)

        def finish(h, m0, m1):
            cols = slice(h * HALF, (h + 1) * HALF)
            new = tile([P, m1 - m0, HALF], F32, "new%d%d" % (h, m0))
            nc.vector.scalar_tensor_tensor(new[:], gated[h][:, m0:m1, :], 0.5, state[:, m0:m1, cols], MULT, ADD)
            nc.sync.dma_start(out.rearrange("(m p) s -> p m s", p=P)[:, m0:m1, cols], new[:])

        load_weights("g", 0, tile([P, PACK * N], F32, "raw_g0")[:], parts=PACK)
        load_weights("f", 0, tile([P, PACK * N], F32, "raw_f0")[:])
        load_words(0)
        load_weights("g", 1, tile([P, PACK * N], F32, "raw_g1")[:])

        picked_bytes = tile([P, S], U8, "picked_bytes")
        nc.vector.tensor_copy(picked_bytes[:], scale_table[:].indirect(offsets[:]))
        planes = tile([P, S], U8, "planes")
        nc.vector.tensor_copy(planes[:].bitcast(I32), picked_bytes[:].bitcast(I32))
        for a in range(PASSES):
            for i in range(RUN_ROWS):
                row = PLANE_STEP * a + i
                nc.sync.dma_start(
                    planes[row + RUN_ROWS : P : QUADRANT, :].bitcast(I32), planes[row + GROUP : P : QUADRANT, :].bitcast(I32)
                )

        load_words(1, reuse="picked_bytes")
        quantize(weave(nc.scalar.copy, "g", 0, 0, ROW_TILES), "g", 0, 0)
        last = tile([P, PACK * N + ROW_TILES * S], F32, "last", reuse="raw_g0")
        load_weights("f", 1, last[:, : PACK * N])
        state = last[:, PACK * N :].rearrange("p (m s) -> p m s", m=ROW_TILES)
        nc.sync.dma_start(state, st.rearrange("(m p) s -> p m s", p=P))
        quantize(weave(nc.scalar.copy, "f", 0, 0, ROW_TILES), "f", 0, 0)

        for h in range(HALVES):
            gather_words(0, h)
            for name in ("g", "f"):
                for m in range(ROW_TILES):
                    product(name, 0, m, h)

        quantize(weave(nc.scalar.copy, "g", 1, 0, ROW_TILES), "g", 1, 0)
        for h in range(HALVES):
            gather_words(1, h)
            for m in range(ROW_TILES):
                product("g", 1, m, h)

        woven_last = [weave(nc.vector.tensor_copy, "f", 1, m, m + 1) for m in range(ROW_TILES)]
        for m in range(ROW_TILES):
            quantize(woven_last[m], "f", 1, m)
        for h in range(HALVES):
            for m in range(ROW_TILES):
                squash("g", m, h)
        for h in range(HALVES):
            for m in range(ROW_TILES):
                product("f", 1, m, h)
                squash("f", m, h)

        subtract(0, reuse="woven_f1_1")
        subtract(1, reuse="woven_f1_0")
        gate(0, 0, ROW_TILES)
        gate(1, 0, 1)
        finish(0, 0, ROW_TILES)
        gate(1, 1, 2)
        finish(1, 0, 1)
        finish(1, 1, 2)
